import numpy as np
import ml_dtypes


def mxq(x, axis, fmt="e4m3"):
    dtype, down = {"e4m3": (ml_dtypes.float8_e4m3fn, 7), "e5m2": (ml_dtypes.float8_e5m2, 14)}[fmt]
    v = np.moveaxis(np.asarray(x, np.float32).astype(ml_dtypes.bfloat16).astype(np.float64), axis, -1)
    blocks = v.reshape(v.shape[:-1] + (-1, 32))
    amax = np.abs(blocks).max(-1, keepdims=True)
    byte = np.maximum(np.where(amax > 0, np.frexp(amax)[1] - 1 + 127, 0) - down, 1)
    scale = np.exp2(byte - 127.0)
    codes = (blocks / scale).astype(np.float32).astype(dtype).astype(np.float64)
    return np.moveaxis((codes * scale).reshape(v.shape), -1, axis)


WIDE = False


def mx_kscale(k):
    if not WIDE:
        return np.ones(k)
    levels = np.array([10, -10, 5, -5, 0])
    if k % 512:
        return np.exp2(np.random.permutation(np.resize(levels, k // 32))).repeat(32)
    a = np.empty((k // 512, 16))
    for p in range(k // 512):
        a[p, :8] = np.random.permutation(np.resize(levels, 8))
        for g in range(8):
            far = levels[np.abs(levels - a[p, g]) >= 10]
            a[p, g + 8] = far[np.random.randint(len(far))]
    return np.exp2(a.ravel()).repeat(32)


def f64(x):
    return np.asarray(x).astype(np.float64)


def striped(idx):
    return np.tile(np.asarray(idx).reshape(-1, 16).T, (8, 1)).astype(np.uint16)


def unstriped(offs):
    return offs[:16].T.reshape(-1).astype(np.int64)


E2M1 = np.array([0.0, 0.5, 1.0, 1.5, 2.0, 3.0, 4.0, 6.0, -0.0, -0.5, -1.0, -1.5, -2.0, -3.0, -4.0, -6.0])


def pack_weight(w, fmt):
    k, n = w.shape
    w = f64(np.asarray(w, np.float32).astype(ml_dtypes.bfloat16)).reshape(k // 32, 32, n)
    amax = np.abs(w).max(1)
    if fmt == "e4m3":
        byte = np.frexp(amax)[1] - 1 + 127 - 7
    else:
        mant, ex = np.frexp(amax / 6.0)
        byte = np.where(mant > 0.5, ex, ex - 1) + 127
    byte = np.clip(np.where(amax > 0, byte, 1), 1, 254)
    scaled = (w * np.exp2(127.0 - byte)[:, None, :]).reshape(k, n).astype(np.float32)
    by_word = np.ascontiguousarray(scaled.reshape(k // 512, 128, 4, n).transpose(0, 1, 3, 2))
    if fmt == "e4m3":
        words = by_word.astype(ml_dtypes.float8_e4m3fn).view(np.uint8)
    else:
        c = by_word.astype(ml_dtypes.float4_e2m1fn).view(np.uint8) & 0xF
        words = (c[..., 0::2] | (c[..., 1::2] << 4)).reshape(k // 512, 128, 2 * n)
    return np.ascontiguousarray(words), np.ascontiguousarray(byte.astype(np.uint8).reshape(k // 512, 16, n))


def unpack_weight(words, scales, fmt):
    g, _, n = scales.shape
    words = np.ascontiguousarray(words).reshape(g, 128, n, -1)
    if fmt == "e4m3":
        vals = words.view(ml_dtypes.float8_e4m3fn).astype(np.float64)
    else:
        nib = np.empty((g, 128, n, 4), np.uint8)
        nib[..., 0::2] = words & 0xF
        nib[..., 1::2] = words >> 4
        vals = E2M1[nib]
    vals = vals * np.repeat(np.exp2(scales.astype(np.float64) - 127.0), 8, axis=1)[..., None]
    return vals.transpose(0, 1, 3, 2).reshape(g * 512, n)


K, C, L, T, N = 512, 512, 512, 1024, 512


def setup_inputs():
    n = np.random.standard_normal
    idx = np.random.randint(0, C, T)
    fk = mx_kscale(K)
    fl = mx_kscale(L)
    xcp = pack_weight(n((K, C)) / fk[:, None], "e2m1")
    xfp = pack_weight(n((L, T)) / fl[:, None], "e4m3")
    wfp = pack_weight(n((L, N)) * 1 / np.sqrt(L) * fl[:, None], "e2m1")
    return {
        "xc_words": xcp[0],
        "xc_scales": xcp[1],
        "wc": (n((K, N)) * 1 / np.sqrt(K) * fk[:, None]).astype(np.float32),
        "xf_words": xfp[0],
        "xf_scales": xfp[1],
        "wf_words": wfp[0],
        "wf_scales": wfp[1],
        "offs": striped(idx),
    }


def reference(xc_words, xc_scales, wc, xf_words, xf_scales, wf_words, wf_scales, offs):
    idx = unstriped(offs)
    xcu = unpack_weight(xc_words, xc_scales, "e2m1")
    xfu = unpack_weight(xf_words, xf_scales, "e4m3")
    wfu = unpack_weight(wf_words, wf_scales, "e2m1")
    wcq = mxq(f64(wc), 0, "e4m3")
    zc = wcq.T @ xcu
    zf = wfu.T @ xfu
    y = np.maximum(zc[:, idx] + zf, 0.0)
    return y

@@ -1,0 +1,198 @@
+from contextlib import ExitStack
+
+import concourse.mybir as mybir
+
+F32 = mybir.dt.float32
+BF16 = mybir.dt.bfloat16
+I32 = mybir.dt.int32
+U32 = mybir.dt.uint32
+U16 = mybir.dt.uint16
+U8 = mybir.dt.uint8
+FP8X4 = mybir.dt.float8_e4m3fn_x4
+FP4X4 = mybir.dt.float4_e2m1fn_x4
+ADD = mybir.AluOpType.add
+RELU = mybir.ActivationFunctionType.Relu
+
+P = 128
+K, C, L, T, N = 512, 512, 512, 1024, 512
+SPARE = 16
+HALF = 512
+FLOPS = 2 * K * N * C + 2 * L * N * T
+
+
+def tile_list_coarse_parents_fine_kernel(tc, xc_words, xc_scales, wc, xf_words, xf_scales, wf_words, wf_scales, offs, out):
+    nc = tc.nc
+    with ExitStack() as ctx:
+        keep = ctx.enter_context(tc.tile_pool(name="keep", bufs=1))
+        psum = ctx.enter_context(tc.psum_pool(name="psum", bufs=1))
+
+        def plane(name, width, engine):
+            t = keep.tile([P, width], U8, name=name, align_bytes=64)
+            engine.memset(t[:].bitcast(I32), 0)
+            return t
+
+        def load_plane(queue, t, rows, quadrants=range(4)):
+            for q in quadrants:
+                queue.dma_start(t[32 * q : 32 * q + 4, :].bitcast(I32), rows[0, 4 * q : 4 * q + 4, :].bitcast(I32))
+
+        xc_plane = plane("xc_plane", C, nc.gpsimd)
+        wf_plane = plane("wf_plane", N, nc.gpsimd)
+        xf_plane = plane("xf_plane", T, nc.vector)
+        zeros = keep.tile([P, SPARE], F32, name="zeros")
+        nc.vector.memset(zeros[:], 0.0)
+
+        wc_rows = wc.rearrange("(p j) n -> p j n", j=4)
+        groups = [(0, 128), (128, 256), (384, 128)]
+        raw = [keep.tile([P, 4, w], F32, name="raw%d" % g) for g, (n0, w) in enumerate(groups)]
+        xc = keep.tile([P, 2 * C], U8, name="xc", align_bytes=64)
+        wf = keep.tile([P, 2 * N], U8, name="wf", align_bytes=64)
+        xf = [keep.tile([P, HALF], U32, name="xf%d" % h, align_bytes=64) for h in range(2)]
+        offsets = keep.tile([P, T // 16], U16, name="offsets")
+        xf_flat = xf_words[0].rearrange("p n t -> p (n t)")
+
+        def load_wc(g):
+            n0, w = groups[g]
+            nc.sync.dma_start(raw[g][:], wc_rows[:, :, n0 : n0 + w])
+
+        def load_xf(h):
+            nc.sync.dma_start(xf[h][:].bitcast(I32), xf_flat[:, 4 * HALF * h : 4 * HALF * (h + 1)].bitcast(I32))
+
+        load_wc(0)
+        nc.sync.dma_start(xc[:].bitcast(I32), xc_words[0].bitcast(I32))
+        load_plane(nc.scalar, xc_plane, xc_scales)
+        load_wc(1)
+        load_wc(2)
+        nc.sync.dma_start(offsets[:], offs)
+        nc.sync.dma_start(wf[:].bitcast(I32), wf_words[0].bitcast(I32))
+        load_plane(nc.sync, wf_plane, wf_scales)
+        load_xf(0)
+        load_xf(1)
+        load_plane(nc.sync, xf_plane, xf_scales)
+
+        zc = [keep.tile([P, C + SPARE], F32, name="zc%d" % j) for j in range(4)]
+        for j in range(4):
+            nc.scalar.activation(zc[j][:, C:], zeros[:], RELU)
+
+        stationary = []
+
+        grouped = {}
+
+        def cast(g, on_scalar=False):
+            n0, w = groups[g]
+            grouped[g] = keep.tile([P, w, 4], BF16, name="grouped%d" % g, align_bytes=64)
+            dst = grouped[g][:].rearrange("p (c i) t -> p c t i", i=4)
+            src = raw[g][:].rearrange("p t (c i) -> p c t i", i=4)
+            if on_scalar:
+                nc.scalar.copy(dst, src)
+            else:
+                nc.vector.tensor_copy(dst, src)
+
+        def quantise(g):
+            n0, w = groups[g]
+            codes = keep.tile([P, w], U32, name="codes%d" % g, align_bytes=64)
+            scales = keep.tile([P, w], U8, name="scales%d" % g, align_bytes=64)
+            nc.vector.quantize_mx(codes[:].bitcast(FP8X4), scales[:], grouped[g][:].rearrange("p c t -> p (c t)"))
+            for m0 in range(0, w, P):
+                stationary.append((codes[:, m0 : m0 + P], scales[:, m0 : m0 + P]))
+
+        def coarse(j, parts=1):
+            codes, scales = stationary[j]
+            w = C // parts
+            for c0 in range(0, C, w):
+                bank = psum.tile([P, C], F32, name="zc_bank", tag="zc_bank", bufs=3)
+                nc.tensor.matmul_mx(
+                    bank[:, :w], codes.bitcast(FP8X4), scales, xc[:, 2 * c0 : 2 * (c0 + w)].bitcast(FP4X4), xc_plane[:, c0 : c0 + w], start=True, stop=True
+                )
+                nc.scalar.copy(zc[j][:, c0 : c0 + w], bank[:, :w])
+
+        zf = {}
+
+        banks = {}
+
+        def fine(j, h):
+            bank = psum.tile([P, HALF], F32, name="zf_bank", tag="zf_bank", bufs=5)
+            nc.tensor.matmul_mx(
+                bank[:],
+                wf[:, 2 * P * j : 2 * P * (j + 1)].bitcast(FP4X4),
+                wf_plane[:, P * j : P * (j + 1)],
+                xf[h][:].bitcast(FP8X4),
+                xf_plane[:, HALF * h : HALF * (h + 1)],
+                start=True,
+                stop=True,
+            )
+            banks[j, h] = bank
+
+        def evacuate(j, h):
+            zf[j, h] = keep.tile([P, HALF], F32, name="zf%d%d" % (j, h))
+            nc.scalar.copy(zf[j, h][:], banks[j, h][:])
+
+        summed = {}
+        picked = {}
+
+        def listed(j, h, a=0, b=HALF):
+            return zc[j][:].indirect(offsets[:, (HALF * h + a) // 16 : (HALF * h + b) // 16])
+
+        def gather_add(j, h, a=0, b=HALF):
+            summed[j, h, a] = keep.tile([P, b - a], F32, name="sum%d%d%d" % (j, h, a))
+            nc.vector.tensor_tensor(summed[j, h, a][:], listed(j, h, a, b), zf[j, h][:, a:b], ADD)
+
+        def gather(j, h):
+            picked[j, h] = keep.tile([P, HALF], F32, name="picked%d%d" % (j, h))
+            nc.vector.tensor_copy(picked[j, h][:], listed(j, h))
+
+        def add(j, h):
+            summed[j, h, 0] = keep.tile([P, HALF], F32, name="sum%d%d" % (j, h))
+            nc.vector.tensor_tensor(summed[j, h, 0][:], banks[j, h][:], picked[j, h][:], ADD)
+
+        def finish(j, h, a=0, b=HALF, on_vector=False):
+            res = keep.tile([P, b - a], F32, name="res%d%d%d" % (j, h, a))
+            if on_vector:
+                nc.vector.tensor_scalar_max(res[:], summed[j, h, a][:], 0.0)
+            else:
+                nc.scalar.activation(res[:], summed[j, h, a][:], RELU)
+            nc.sync.dma_start(out[P * j : P * (j + 1), HALF * h + a : HALF * h + b], res[:])
+
+        cast(0)
+        quantise(0)
+        coarse(0, parts=2)
+        cast(1)
+        quantise(1)
+        cast(2, on_scalar=True)
+        gather(0, 0)
+        coarse(1)
+        quantise(2)
+        gather(0, 1)
+        coarse(2)
+        fine(1, 0)
+        evacuate(1, 0)
+        fine(0, 0)
+        fine(0, 1)
+        add(0, 0)
+        add(0, 1)
+        fine(1, 1)
+        evacuate(1, 1)
+        gather_add(1, 0)
+        coarse(3)
+        finish(0, 0)
+        fine(2, 0)
+        evacuate(2, 0)
+        gather_add(1, 1)
+        finish(0, 1)
+        fine(2, 1)
+        evacuate(2, 1)
+        gather_add(2, 0)
+        finish(1, 0)
+        fine(3, 0)
+        evacuate(3, 0)
+        gather_add(2, 1)
+        finish(1, 1)
+        fine(3, 1)
+        evacuate(3, 1)
+        gather_add(3, 0)
+        finish(2, 0)
+        finish(2, 1)
+        gather_add(3, 1, 0, 256)
+        finish(3, 0)
+        gather_add(3, 1, 256, 512)
+        finish(3, 1, 0, 256)
+        finish(3, 1, 256, 512)

@@ -28,7 +28,6 @@ def tile_list_coarse_parents_fine_kernel(tc, xc_words, xc_scales, wc, xf_words, 
 
         def plane(name, width, engine):
             t = keep.tile([P, width], U8, name=name, align_bytes=64)
-            engine.memset(t[:].bitcast(I32), 0)
             return t
 
         def load_plane(queue, t, rows, quadrants=range(4)):
@@ -54,20 +53,21 @@ def tile_list_coarse_parents_fine_kernel(tc, xc_words, xc_scales, wc, xf_words, 
             n0, w = groups[g]
             nc.sync.dma_start(raw[g][:], wc_rows[:, :, n0 : n0 + w])
 
-        def load_xf(h):
-            nc.sync.dma_start(xf[h][:].bitcast(I32), xf_flat[:, 4 * HALF * h : 4 * HALF * (h + 1)].bitcast(I32))
+        def load_xf(h, queue=nc.sync):
+            queue.dma_start(xf[h][:].bitcast(I32), xf_flat[:, 4 * HALF * h : 4 * HALF * (h + 1)].bitcast(I32))
 
         load_wc(0)
         nc.sync.dma_start(xc[:].bitcast(I32), xc_words[0].bitcast(I32))
-        load_plane(nc.scalar, xc_plane, xc_scales)
-        load_wc(1)
-        load_wc(2)
+        load_plane(nc.sync, xc_plane, xc_scales)
+        nc.gpsimd.dma_start(wf[:].bitcast(I32), wf_words[0].bitcast(I32))
+        load_xf(0, nc.gpsimd)
+        load_plane(nc.gpsimd, xf_plane, xf_scales, [3])
         nc.sync.dma_start(offsets[:], offs)
-        nc.sync.dma_start(wf[:].bitcast(I32), wf_words[0].bitcast(I32))
+        load_wc(1)
         load_plane(nc.sync, wf_plane, wf_scales)
-        load_xf(0)
+        load_plane(nc.sync, xf_plane, xf_scales, [0, 1, 2])
         load_xf(1)
-        load_plane(nc.sync, xf_plane, xf_scales)
+        load_wc(2)
 
         zc = [keep.tile([P, C + SPARE], F32, name="zc%d" % j) for j in range(4)]
         for j in range(4):
@@ -79,7 +79,7 @@ def tile_list_coarse_parents_fine_kernel(tc, xc_words, xc_scales, wc, xf_words, 
 
         def cast(g, on_scalar=False):
             n0, w = groups[g]
-            grouped[g] = keep.tile([P, w, 4], BF16, name="grouped%d" % g, align_bytes=64)
+            grouped[g] = keep.tile([P, w, 4], BF16, name="grouped%d" % g, tag="grouped%d" % g, align_bytes=64)
             dst = grouped[g][:].rearrange("p (c i) t -> p c t i", i=4)
             src = raw[g][:].rearrange("p t (c i) -> p c t i", i=4)
             if on_scalar:
@@ -136,8 +136,8 @@ def tile_list_coarse_parents_fine_kernel(tc, xc_words, xc_scales, wc, xf_words, 
             summed[j, h, a] = keep.tile([P, b - a], F32, name="sum%d%d%d" % (j, h, a))
             nc.vector.tensor_tensor(summed[j, h, a][:], listed(j, h, a, b), zf[j, h][:, a:b], ADD)
 
-        def gather(j, h):
-            picked[j, h] = keep.tile([P, HALF], F32, name="picked%d%d" % (j, h))
+        def gather(j, h, tag):
+            picked[j, h] = keep.tile([P, HALF], F32, name="picked%d%d" % (j, h), tag=tag, align_bytes=64)
             nc.vector.tensor_copy(picked[j, h][:], listed(j, h))
 
         def add(j, h):
@@ -157,39 +157,39 @@ def tile_list_coarse_parents_fine_kernel(tc, xc_words, xc_scales, wc, xf_words, 
         coarse(0, parts=2)
         cast(1)
         quantise(1)
-        cast(2, on_scalar=True)
-        gather(0, 0)
+        gather(0, 0, "grouped1")
         coarse(1)
-        quantise(2)
-        gather(0, 1)
-        coarse(2)
+        fine(0, 0)
         fine(1, 0)
         evacuate(1, 0)
-        fine(0, 0)
-        fine(0, 1)
         add(0, 0)
-        add(0, 1)
-        fine(1, 1)
-        evacuate(1, 1)
+        coarse(2)
         gather_add(1, 0)
-        coarse(3)
-        finish(0, 0)
         fine(2, 0)
         evacuate(2, 0)
-        gather_add(1, 1)
-        finish(0, 1)
-        fine(2, 1)
-        evacuate(2, 1)
+        fine(0, 1)
+        finish(0, 0)
+        evacuate(0, 1)
         gather_add(2, 0)
+        cast(2)
+        quantise(2)
+        fine(1, 1)
         finish(1, 0)
+        evacuate(1, 1)
+        gather_add(0, 1)
+        fine(2, 1)
+        finish(2, 0)
+        evacuate(2, 1)
+        gather_add(1, 1)
+        coarse(3)
         fine(3, 0)
         evacuate(3, 0)
         gather_add(2, 1)
-        finish(1, 1)
+        finish(0, 1)
         fine(3, 1)
         evacuate(3, 1)
         gather_add(3, 0)
-        finish(2, 0)
+        finish(1, 1)
         finish(2, 1)
         gather_add(3, 1, 0, 256)
         finish(3, 0)

@@ -11,6 +11,7 @@ U8 = mybir.dt.uint8
 FP8X4 = mybir.dt.float8_e4m3fn_x4
 FP4X4 = mybir.dt.float4_e2m1fn_x4
 ADD = mybir.AluOpType.add
+MULT = mybir.AluOpType.mult
 RELU = mybir.ActivationFunctionType.Relu
 
 P = 128
@@ -26,74 +27,71 @@ def tile_list_coarse_parents_fine_kernel(tc, xc_words, xc_scales, wc, xf_words, 
         keep = ctx.enter_context(tc.tile_pool(name="keep", bufs=1))
         psum = ctx.enter_context(tc.psum_pool(name="psum", bufs=1))
 
-        def plane(name, width, engine):
-            t = keep.tile([P, width], U8, name=name, align_bytes=64)
-            return t
+        xc_plane = keep.tile([P, C], U8, name="xc_plane", align_bytes=64)
+        wf_plane = keep.tile([P, N], U8, name="wf_plane", align_bytes=64)
+        xf_plane = keep.tile([P, T], U8, name="xf_plane", align_bytes=64)
+        xc = keep.tile([P, 2 * C], U8, name="xc", align_bytes=64)
+        wf = keep.tile([P, 2 * N], U8, name="wf", align_bytes=64)
+        xf = [keep.tile([P, HALF], U32, name="xf%d" % h, align_bytes=64) for h in range(2)]
+        offsets = keep.tile([P, T // 16], U16, name="offsets")
+        zeros = keep.tile([P, SPARE], F32, name="zeros")
+        nc.vector.memset(zeros[:], 0.0)
+
+        wc_rows = wc.rearrange("(p j) n -> p j n", j=4)
+        xf_flat = xf_words[0].rearrange("p n t -> p (n t)")
+        raw = {}
 
         def load_plane(queue, t, rows, quadrants=range(4)):
             for q in quadrants:
                 queue.dma_start(t[32 * q : 32 * q + 4, :].bitcast(I32), rows[0, 4 * q : 4 * q + 4, :].bitcast(I32))
 
-        xc_plane = plane("xc_plane", C, nc.gpsimd)
-        wf_plane = plane("wf_plane", N, nc.gpsimd)
-        xf_plane = plane("xf_plane", T, nc.vector)
-        zeros = keep.tile([P, SPARE], F32, name="zeros")
-        nc.vector.memset(zeros[:], 0.0)
-
-        wc_rows = wc.rearrange("(p j) n -> p j n", j=4)
-        groups = [(0, 128), (128, 256), (384, 128)]
-        raw = [keep.tile([P, 4, w], F32, name="raw%d" % g) for g, (n0, w) in enumerate(groups)]
-        xc = keep.tile([P, 2 * C], U8, name="xc", align_bytes=64)
-        wf = keep.tile([P, 2 * N], U8, name="wf", align_bytes=64)
-        xf = [keep.tile([P, HALF], U32, name="xf%d" % h, align_bytes=64) for h in range(2)]
-        offsets = keep.tile([P, T // 16], U16, name="offsets")
-        xf_flat = xf_words[0].rearrange("p n t -> p (n t)")
-
-        def load_wc(g):
-            n0, w = groups[g]
-            nc.sync.dma_start(raw[g][:], wc_rows[:, :, n0 : n0 + w])
-
         def load_xf(h, queue=nc.sync):
             queue.dma_start(xf[h][:].bitcast(I32), xf_flat[:, 4 * HALF * h : 4 * HALF * (h + 1)].bitcast(I32))
 
-        load_wc(0)
+        def load_wc(j0, count, queue=nc.sync):
+            t = keep.tile([P, 4, P * count], F32, name="raw%d" % j0, tag="raw%d" % j0, align_bytes=64)
+            queue.dma_start(t[:], wc_rows[:, :, P * j0 : P * (j0 + count)])
+            raw[j0] = t
+
+        load_wc(0, 1)
         nc.sync.dma_start(xc[:].bitcast(I32), xc_words[0].bitcast(I32))
         load_plane(nc.sync, xc_plane, xc_scales)
-        nc.gpsimd.dma_start(wf[:].bitcast(I32), wf_words[0].bitcast(I32))
-        load_xf(0, nc.gpsimd)
-        load_plane(nc.gpsimd, xf_plane, xf_scales, [3])
+        load_plane(nc.gpsimd, xf_plane, xf_scales, [3, 2])
+        load_xf(1, nc.gpsimd)
         nc.sync.dma_start(offsets[:], offs)
-        load_wc(1)
-        load_plane(nc.sync, wf_plane, wf_scales)
-        load_plane(nc.sync, xf_plane, xf_scales, [0, 1, 2])
-        load_xf(1)
-        load_wc(2)
+        load_wc(1, 1)
+        load_plane(nc.sync, wf_plane, wf_scales, [0, 1])
+        nc.sync.dma_start(wf[:].bitcast(I32), wf_words[0].bitcast(I32))
+        load_xf(0)
+        load_plane(nc.sync, wf_plane, wf_scales, [2, 3])
+        load_plane(nc.sync, xf_plane, xf_scales, [0, 1])
+        load_wc(2, 1)
+        load_wc(3, 1)
 
         zc = [keep.tile([P, C + SPARE], F32, name="zc%d" % j) for j in range(4)]
         for j in range(4):
             nc.scalar.activation(zc[j][:, C:], zeros[:], RELU)
 
-        stationary = []
+        grouped, stationary, banks, zf, summed, picked = {}, {}, {}, {}, {}, {}
 
-        grouped = {}
-
-        def cast(g, on_scalar=False):
-            n0, w = groups[g]
-            grouped[g] = keep.tile([P, w, 4], BF16, name="grouped%d" % g, tag="grouped%d" % g, align_bytes=64)
-            dst = grouped[g][:].rearrange("p (c i) t -> p c t i", i=4)
-            src = raw[g][:].rearrange("p t (c i) -> p c t i", i=4)
-            if on_scalar:
-                nc.scalar.copy(dst, src)
+        def cast(j0, count, engine):
+            grouped[j0] = keep.tile([P, P * count, 4], BF16, name="grouped%d" % j0, tag="grouped%d" % j0, align_bytes=64)
+            if engine == "gpsimd":
+                for i in range(count):
+                    nc.gpsimd.tensor_scalar(
+                        grouped[j0][:, P * i : P * (i + 1)], raw[j0 + i][:].rearrange("p t c -> p c t"), 1.0, 0.0, MULT, ADD
+                    )
             else:
-                nc.vector.tensor_copy(dst, src)
+                nc.vector.tensor_copy(
+                    grouped[j0][:].rearrange("p (c i) t -> p c t i", i=4), raw[j0][:].rearrange("p t (c i) -> p c t i", i=4)
+                )
 
-        def quantise(g):
-            n0, w = groups[g]
-            codes = keep.tile([P, w], U32, name="codes%d" % g, align_bytes=64)
-            scales = keep.tile([P, w], U8, name="scales%d" % g, align_bytes=64)
-            nc.vector.quantize_mx(codes[:].bitcast(FP8X4), scales[:], grouped[g][:].rearrange("p c t -> p (c t)"))
-            for m0 in range(0, w, P):
-                stationary.append((codes[:, m0 : m0 + P], scales[:, m0 : m0 + P]))
+        def quantise(j0, count):
+            codes = keep.tile([P, P * count], U32, name="codes%d" % j0, align_bytes=64)
+            scales = keep.tile([P, P * count], U8, name="scales%d" % j0, align_bytes=64)
+            nc.vector.quantize_mx(codes[:].bitcast(FP8X4), scales[:], grouped[j0][:].rearrange("p c t -> p (c t)"))
+            for i in range(count):
+                stationary[j0 + i] = (codes[:, P * i : P * (i + 1)], scales[:, P * i : P * (i + 1)])
 
         def coarse(j, parts=1):
             codes, scales = stationary[j]
@@ -105,14 +103,10 @@ def tile_list_coarse_parents_fine_kernel(tc, xc_words, xc_scales, wc, xf_words, 
                 )
                 nc.scalar.copy(zc[j][:, c0 : c0 + w], bank[:, :w])
 
-        zf = {}
-
-        banks = {}
-
-        def fine(j, h):
-            bank = psum.tile([P, HALF], F32, name="zf_bank", tag="zf_bank", bufs=5)
+        def fine(j, h, tag="zf_bank"):
+            banks[j, h] = psum.tile([P, HALF], F32, name=tag, tag=tag, bufs=5)
             nc.tensor.matmul_mx(
-                bank[:],
+                banks[j, h][:],
                 wf[:, 2 * P * j : 2 * P * (j + 1)].bitcast(FP4X4),
                 wf_plane[:, P * j : P * (j + 1)],
                 xf[h][:].bitcast(FP8X4),
@@ -120,20 +114,18 @@ def tile_list_coarse_parents_fine_kernel(tc, xc_words, xc_scales, wc, xf_words, 
                 start=True,
                 stop=True,
             )
-            banks[j, h] = bank
 
-        def evacuate(j, h):
-            zf[j, h] = keep.tile([P, HALF], F32, name="zf%d%d" % (j, h))
+        def evacuate(j, h, tag=None):
+            name = "zf%d%d" % (j, h)
+            zf[j, h] = keep.tile([P, HALF], F32, name=name, tag=tag or name, align_bytes=64)
             nc.scalar.copy(zf[j, h][:], banks[j, h][:])
-
-        summed = {}
-        picked = {}
 
         def listed(j, h, a=0, b=HALF):
             return zc[j][:].indirect(offsets[:, (HALF * h + a) // 16 : (HALF * h + b) // 16])
 
-        def gather_add(j, h, a=0, b=HALF):
-            summed[j, h, a] = keep.tile([P, b - a], F32, name="sum%d%d%d" % (j, h, a))
+        def gather_add(j, h, a=0, b=HALF, tag=None):
+            name = "sum%d%d%d" % (j, h, a)
+            summed[j, h, a] = keep.tile([P, b - a], F32, name=name, tag=tag or name, align_bytes=64)
             nc.vector.tensor_tensor(summed[j, h, a][:], listed(j, h, a, b), zf[j, h][:, a:b], ADD)
 
         def gather(j, h, tag):
@@ -152,47 +144,47 @@ def tile_list_coarse_parents_fine_kernel(tc, xc_words, xc_scales, wc, xf_words, 
                 nc.scalar.activation(res[:], summed[j, h, a][:], RELU)
             nc.sync.dma_start(out[P * j : P * (j + 1), HALF * h + a : HALF * h + b], res[:])
 
-        cast(0)
-        quantise(0)
+        cast(0, 1, "vector")
+        quantise(0, 1)
         coarse(0, parts=2)
-        cast(1)
-        quantise(1)
+        cast(1, 1, "vector")
+        quantise(1, 1)
         gather(0, 0, "grouped1")
         coarse(1)
+        cast(2, 2, "gpsimd")
+        gather(1, 0, "pick_b")
         fine(0, 0)
         fine(1, 0)
-        evacuate(1, 0)
+        fine(0, 1)
+        evacuate(0, 1)
+        fine(1, 1)
+        evacuate(1, 1)
         add(0, 0)
-        coarse(2)
-        gather_add(1, 0)
+        add(1, 0)
         fine(2, 0)
         evacuate(2, 0)
-        fine(0, 1)
         finish(0, 0)
-        evacuate(0, 1)
-        gather_add(2, 0)
-        cast(2)
-        quantise(2)
-        fine(1, 1)
-        finish(1, 0)
-        evacuate(1, 1)
         gather_add(0, 1)
+        quantise(2, 2)
+        finish(1, 0)
         fine(2, 1)
-        finish(2, 0)
         evacuate(2, 1)
-        gather_add(1, 1)
+        coarse(2)
+        gather_add(1, 1, tag="grouped2")
+        finish(0, 1)
         coarse(3)
+        gather_add(2, 0)
         fine(3, 0)
         evacuate(3, 0)
+        finish(1, 1)
         gather_add(2, 1)
-        finish(0, 1)
         fine(3, 1)
         evacuate(3, 1)
+        finish(2, 0)
         gather_add(3, 0)
-        finish(1, 1)
         finish(2, 1)
-        gather_add(3, 1, 0, 256)
+        gather_add(3, 1, 0, 320)
         finish(3, 0)
-        gather_add(3, 1, 256, 512)
-        finish(3, 1, 0, 256)
-        finish(3, 1, 256, 512)
+        gather_add(3, 1, 320, 512)
+        finish(3, 1, 0, 320)
+        finish(3, 1, 320, 512)

from contextlib import ExitStack

import concourse.mybir as mybir

F32 = mybir.dt.float32
BF16 = mybir.dt.bfloat16
I32 = mybir.dt.int32
U32 = mybir.dt.uint32
U16 = mybir.dt.uint16
U8 = mybir.dt.uint8
FP8X4 = mybir.dt.float8_e4m3fn_x4
FP4X4 = mybir.dt.float4_e2m1fn_x4
ADD = mybir.AluOpType.add
MULT = mybir.AluOpType.mult
RELU = mybir.ActivationFunctionType.Relu

P = 128
K, C, L, T, N = 512, 512, 512, 1024, 512
SPARE = 16
HALF = 512
FLOPS = 2 * K * N * C + 2 * L * N * T


def tile_list_coarse_parents_fine_kernel(tc, xc_words, xc_scales, wc, xf_words, xf_scales, wf_words, wf_scales, offs, out):
    nc = tc.nc
    with ExitStack() as ctx:
        keep = ctx.enter_context(tc.tile_pool(name="keep", bufs=1))
        psum = ctx.enter_context(tc.psum_pool(name="psum", bufs=1))

        xc_plane = keep.tile([P, C], U8, name="xc_plane", align_bytes=64)
        wf_plane = keep.tile([P, N], U8, name="wf_plane", align_bytes=64)
        xf_plane = keep.tile([P, T], U8, name="xf_plane", align_bytes=64)
        xc = keep.tile([P, 2 * C], U8, name="xc", align_bytes=64)
        wf = keep.tile([P, 2 * N], U8, name="wf", align_bytes=64)
        xf = [keep.tile([P, HALF], U32, name="xf%d" % h, align_bytes=64) for h in range(2)]
        offsets = keep.tile([P, T // 16], U16, name="offsets")
        zeros = keep.tile([P, SPARE], F32, name="zeros")
        nc.vector.memset(zeros[:], 0.0)

        wc_rows = wc.rearrange("(p j) n -> p j n", j=4)
        xf_flat = xf_words[0].rearrange("p n t -> p (n t)")
        raw = {}

        def load_plane(queue, t, rows, quadrants=range(4)):
            for q in quadrants:
                queue.dma_start(t[32 * q : 32 * q + 4, :].bitcast(I32), rows[0, 4 * q : 4 * q + 4, :].bitcast(I32))

        def load_xf(h, queue=nc.sync):
            queue.dma_start(xf[h][:].bitcast(I32), xf_flat[:, 4 * HALF * h : 4 * HALF * (h + 1)].bitcast(I32))

        def load_wc(j0, count, queue=nc.sync):
            t = keep.tile([P, 4, P * count], F32, name="raw%d" % j0, tag="raw%d" % j0, align_bytes=64)
            queue.dma_start(t[:], wc_rows[:, :, P * j0 : P * (j0 + count)])
            raw[j0] = t

        load_wc(0, 1)
        nc.sync.dma_start(xc[:].bitcast(I32), xc_words[0].bitcast(I32))
        load_plane(nc.sync, xc_plane, xc_scales)
        load_plane(nc.gpsimd, xf_plane, xf_scales, [3, 2])
        load_xf(1, nc.gpsimd)
        nc.sync.dma_start(offsets[:], offs)
        load_wc(1, 1)
        load_plane(nc.sync, wf_plane, wf_scales, [0, 1])
        nc.sync.dma_start(wf[:].bitcast(I32), wf_words[0].bitcast(I32))
        load_xf(0)
        load_plane(nc.sync, wf_plane, wf_scales, [2, 3])
        load_plane(nc.sync, xf_plane, xf_scales, [0, 1])
        load_wc(2, 1)
        load_wc(3, 1)

        zc = [keep.tile([P, C + SPARE], F32, name="zc%d" % j) for j in range(4)]
        for j in range(4):
            nc.scalar.activation(zc[j][:, C:], zeros[:], RELU)

        grouped, stationary, banks, zf, summed, picked = {}, {}, {}, {}, {}, {}

        def cast(j0, count, engine):
            grouped[j0] = keep.tile([P, P * count, 4], BF16, name="grouped%d" % j0, tag="grouped%d" % j0, align_bytes=64)
            if engine == "gpsimd":
                for i in range(count):
                    nc.gpsimd.tensor_scalar(
                        grouped[j0][:, P * i : P * (i + 1)], raw[j0 + i][:].rearrange("p t c -> p c t"), 1.0, 0.0, MULT, ADD
                    )
            else:
                nc.vector.tensor_copy(
                    grouped[j0][:].rearrange("p (c i) t -> p c t i", i=4), raw[j0][:].rearrange("p t (c i) -> p c t i", i=4)
                )

        def quantise(j0, count):
            codes = keep.tile([P, P * count], U32, name="codes%d" % j0, align_bytes=64)
            scales = keep.tile([P, P * count], U8, name="scales%d" % j0, align_bytes=64)
            nc.vector.quantize_mx(codes[:].bitcast(FP8X4), scales[:], grouped[j0][:].rearrange("p c t -> p (c t)"))
            for i in range(count):
                stationary[j0 + i] = (codes[:, P * i : P * (i + 1)], scales[:, P * i : P * (i + 1)])

        def coarse(j, parts=1):
            codes, scales = stationary[j]
            w = C // parts
            for c0 in range(0, C, w):
                bank = psum.tile([P, C], F32, name="zc_bank", tag="zc_bank", bufs=3)
                nc.tensor.matmul_mx(
                    bank[:, :w], codes.bitcast(FP8X4), scales, xc[:, 2 * c0 : 2 * (c0 + w)].bitcast(FP4X4), xc_plane[:, c0 : c0 + w], start=True, stop=True
                )
                nc.scalar.copy(zc[j][:, c0 : c0 + w], bank[:, :w])

        def fine(j, h, tag="zf_bank"):
            banks[j, h] = psum.tile([P, HALF], F32, name=tag, tag=tag, bufs=5)
            nc.tensor.matmul_mx(
                banks[j, h][:],
                wf[:, 2 * P * j : 2 * P * (j + 1)].bitcast(FP4X4),
                wf_plane[:, P * j : P * (j + 1)],
                xf[h][:].bitcast(FP8X4),
                xf_plane[:, HALF * h : HALF * (h + 1)],
                start=True,
                stop=True,
            )

        def evacuate(j, h, tag=None):
            name = "zf%d%d" % (j, h)
            zf[j, h] = keep.tile([P, HALF], F32, name=name, tag=tag or name, align_bytes=64)
            nc.scalar.copy(zf[j, h][:], banks[j, h][:])

        def listed(j, h, a=0, b=HALF):
            return zc[j][:].indirect(offsets[:, (HALF * h + a) // 16 : (HALF * h + b) // 16])

        def gather_add(j, h, a=0, b=HALF, tag=None):
            name = "sum%d%d%d" % (j, h, a)
            summed[j, h, a] = keep.tile([P, b - a], F32, name=name, tag=tag or name, align_bytes=64)
            nc.vector.tensor_tensor(summed[j, h, a][:], listed(j, h, a, b), zf[j, h][:, a:b], ADD)

        def gather(j, h, tag):
            picked[j, h] = keep.tile([P, HALF], F32, name="picked%d%d" % (j, h), tag=tag, align_bytes=64)
            nc.vector.tensor_copy(picked[j, h][:], listed(j, h))

        def add(j, h):
            summed[j, h, 0] = keep.tile([P, HALF], F32, name="sum%d%d" % (j, h))
            nc.vector.tensor_tensor(summed[j, h, 0][:], banks[j, h][:], picked[j, h][:], ADD)

        def finish(j, h, a=0, b=HALF, on_vector=False):
            res = keep.tile([P, b - a], F32, name="res%d%d%d" % (j, h, a))
            if on_vector:
                nc.vector.tensor_scalar_max(res[:], summed[j, h, a][:], 0.0)
            else:
                nc.scalar.activation(res[:], summed[j, h, a][:], RELU)
            nc.sync.dma_start(out[P * j : P * (j + 1), HALF * h + a : HALF * h + b], res[:])

        cast(0, 1, "vector")
        quantise(0, 1)
        coarse(0, parts=2)
        cast(1, 1, "vector")
        quantise(1, 1)
        gather(0, 0, "grouped1")
        coarse(1)
        cast(2, 2, "gpsimd")
        gather(1, 0, "pick_b")
        fine(0, 0)
        fine(1, 0)
        fine(0, 1)
        evacuate(0, 1)
        fine(1, 1)
        evacuate(1, 1)
        add(0, 0)
        add(1, 0)
        fine(2, 0)
        evacuate(2, 0)
        finish(0, 0)
        gather_add(0, 1)
        quantise(2, 2)
        finish(1, 0)
        fine(2, 1)
        evacuate(2, 1)
        coarse(2)
        gather_add(1, 1, tag="grouped2")
        finish(0, 1)
        coarse(3)
        gather_add(2, 0)
        fine(3, 0)
        evacuate(3, 0)
        finish(1, 1)
        gather_add(2, 1)
        fine(3, 1)
        evacuate(3, 1)
        finish(2, 0)
        gather_add(3, 0)
        finish(2, 1)
        gather_add(3, 1, 0, 320)
        finish(3, 0)
        gather_add(3, 1, 320, 512)
        finish(3, 1, 0, 320)
        finish(3, 1, 320, 512)
